import numpy as np
import ml_dtypes


def mxq(x, axis, fmt="e4m3"):
    dtype, down = {"e4m3": (ml_dtypes.float8_e4m3fn, 7), "e5m2": (ml_dtypes.float8_e5m2, 14)}[fmt]
    v = np.moveaxis(np.asarray(x, np.float32).astype(ml_dtypes.bfloat16).astype(np.float64), axis, -1)
    blocks = v.reshape(v.shape[:-1] + (-1, 32))
    amax = np.abs(blocks).max(-1, keepdims=True)
    byte = np.maximum(np.where(amax > 0, np.frexp(amax)[1] - 1 + 127, 0) - down, 1)
    scale = np.exp2(byte - 127.0)
    codes = (blocks / scale).astype(np.float32).astype(dtype).astype(np.float64)
    return np.moveaxis((codes * scale).reshape(v.shape), -1, axis)


WIDE = False


def mx_kscale(k):
    if not WIDE:
        return np.ones(k)
    levels = np.array([10, -10, 5, -5, 0])
    if k % 512:
        return np.exp2(np.random.permutation(np.resize(levels, k // 32))).repeat(32)
    a = np.empty((k // 512, 16))
    for p in range(k // 512):
        a[p, :8] = np.random.permutation(np.resize(levels, 8))
        for g in range(8):
            far = levels[np.abs(levels - a[p, g]) >= 10]
            a[p, g + 8] = far[np.random.randint(len(far))]
    return np.exp2(a.ravel()).repeat(32)


def f64(x):
    return np.asarray(x).astype(np.float64)


def striped(idx):
    return np.tile(idx.reshape(-1, 16).T, (8, 1)).astype(np.uint16)


def unstriped(offs):
    return offs[:16].T.reshape(-1).astype(np.int64)


E2M1 = np.array([0.0, 0.5, 1.0, 1.5, 2.0, 3.0, 4.0, 6.0, -0.0, -0.5, -1.0, -1.5, -2.0, -3.0, -4.0, -6.0])


def pack_weight(w, fmt):
    k, n = w.shape
    w = f64(np.asarray(w, np.float32).astype(ml_dtypes.bfloat16)).reshape(k // 32, 32, n)
    amax = np.abs(w).max(1)
    if fmt == "e4m3":
        byte = np.frexp(amax)[1] - 1 + 127 - 7
    else:
        mant, ex = np.frexp(amax / 6.0)
        byte = np.where(mant > 0.5, ex, ex - 1) + 127
    byte = np.clip(np.where(amax > 0, byte, 1), 1, 254)
    scaled = (w * np.exp2(127.0 - byte)[:, None, :]).reshape(k, n).astype(np.float32)
    by_word = np.ascontiguousarray(scaled.reshape(k // 512, 128, 4, n).transpose(0, 1, 3, 2))
    if fmt == "e4m3":
        words = by_word.astype(ml_dtypes.float8_e4m3fn).view(np.uint8)
    else:
        c = by_word.astype(ml_dtypes.float4_e2m1fn).view(np.uint8) & 0xF
        words = (c[..., 0::2] | (c[..., 1::2] << 4)).reshape(k // 512, 128, 2 * n)
    return np.ascontiguousarray(words), np.ascontiguousarray(byte.astype(np.uint8).reshape(k // 512, 16, n))


def unpack_weight(words, scales, fmt):
    g, _, n = scales.shape
    words = np.ascontiguousarray(words).reshape(g, 128, n, -1)
    if fmt == "e4m3":
        vals = words.view(ml_dtypes.float8_e4m3fn).astype(np.float64)
    else:
        nib = np.empty((g, 128, n, 4), np.uint8)
        nib[..., 0::2] = words & 0xF
        nib[..., 1::2] = words >> 4
        vals = E2M1[nib]
    vals = vals * np.repeat(np.exp2(scales.astype(np.float64) - 127.0), 8, axis=1)[..., None]
    return vals.transpose(0, 1, 3, 2).reshape(g * 512, n)


def gelu(v):
    return 0.5 * v * (1.0 + np.tanh(np.sqrt(2.0 / np.pi) * (v + 0.044715 * v**3)))


def bf(x):
    return np.asarray(x, np.float32).astype(ml_dtypes.bfloat16)

def planes(Y):
    n, m = Y.shape
    b = f64(bf(Y)).reshape(n // 32, 32, m)
    amax = np.abs(b).max(1)
    byte = np.clip(np.where(amax > 0, np.frexp(amax)[1] - 1 + 127 - 7, 1), 1, 254)
    codes = (b * np.exp2(127.0 - byte)[:, None, :]).reshape(n, m).astype(np.float32).astype(ml_dtypes.float8_e4m3fn).view(np.uint8)
    words = codes.reshape(n // 512, 128, 4, m).transpose(0, 1, 3, 2)
    return np.ascontiguousarray(words), np.ascontiguousarray(byte.astype(np.uint8).reshape(n // 512, 16, m))


K, K2, T, T2, S, H, N = 1024, 512, 2048, 4096, 1024, 1024, 1024

def setup_inputs():
    n = np.random.standard_normal
    s = mx_kscale(K)[:, None]
    s2 = mx_kscale(K2)[:, None]
    u = mx_kscale(H)[:, None]
    e = np.exp(0.8 * n(N))
    tab_words, tab_scales = pack_weight(n((K, T)) * s, "e4m3")
    tab2_words, tab2_scales = pack_weight(n((K2, T2)) * s2, "e4m3")
    w4_words, w4_scales = pack_weight(0.34 * n((K2, H)) / np.sqrt(K2) / s2, "e2m1")
    return {
        "tab_words": tab_words, "tab_scales": tab_scales,
        "tab2_words": tab2_words, "tab2_scales": tab2_scales,
        "offs": striped(np.random.permutation(T)[:S]),
        "offs2": striped(np.random.permutation(T2)[:S]),
        "w1": (0.34 * n((K, H)) / np.sqrt(K) / s).astype(np.float32),
        "w4_words": w4_words, "w4_scales": w4_scales,
        "phi": (0.1 * n(H)).astype(np.float32),
        "b": (np.exp(0.3 * n(H)) * u[:, 0]).astype(np.float32),
        "wi": (1.5 * n((H, N)) / np.sqrt(H) / u * e).astype(np.float32),
        "p0": (0.5 * n(N) * e).astype(np.float32),
    }

def reference(tab_words, tab_scales, tab2_words, tab2_scales, offs, offs2, w1, w4_words, w4_scales, phi, b, wi, p0):
    v = unpack_weight(tab_words, tab_scales, "e4m3")[:, unstriped(offs)]
    v2 = unpack_weight(tab2_words, tab2_scales, "e4m3")[:, unstriped(offs2)]
    w4 = unpack_weight(w4_words, w4_scales, "e2m1")
    ts = mxq(f64(w1), 0, "e4m3").T @ v
    tr = w4.T @ v2
    h = f64(b)[:, None] * np.sin(ts - tr - f64(phi)[:, None])
    y = (mxq(f64(wi), 0, "e4m3").T @ mxq(h, 0, "e4m3")) + f64(p0)[:, None]
    words, scales = planes(y)
    return y, words, scales

from contextlib import ExitStack

import concourse.mybir as mybir

K, K2, T, T2, S, H, N = 1024, 512, 2048, 4096, 1024, 1024, 1024
FLOPS = 2 * (K + K2) * H * S + 2 * H * N * S

F32 = mybir.dt.float32
BF16 = mybir.dt.bfloat16
I32 = mybir.dt.int32
U32 = mybir.dt.uint32
U16 = mybir.dt.uint16
U8 = mybir.dt.uint8
FP8X4 = mybir.dt.float8_e4m3fn_x4
FP4X4 = mybir.dt.float4_e2m1fn_x4
ACT = mybir.ActivationFunctionType
ALU = mybir.AluOpType

P = 128
PACK = 4
GROUP = P * PACK
QUADS = 4
COLS = 512
LIST_ROWS = 16


def tile_list_tie_line_injection_kernel(
    tc, tab_words, tab_scales, tab2_words, tab2_scales, offs, offs2, w1, w4_words, w4_scales, phi, b, wi, p0,
    out_0, out_1, out_2,
):
    nc = tc.nc
    with ExitStack() as ctx:
        keep = ctx.enter_context(tc.tile_pool(name="keep", bufs=1))
        ring = ctx.enter_context(tc.tile_pool(name="ring", bufs=2))
        psum = ctx.enter_context(tc.psum_pool(name="psum", bufs=8))

        list1 = keep.tile([P, S // LIST_ROWS], U16, name="list1")
        list2 = keep.tile([P, S // LIST_ROWS], U16, name="list2")
        v_words = [keep.tile([P, T], U32, name="v_words%d" % a) for a in range(2)]
        v2_words = keep.tile([P, T2], U32, name="v2_words")
        v_scales = keep.tile([P, T], U8, name="v_scales")
        v2_scales = keep.tile([P, T2], U8, name="v2_scales")
        w4_raw = keep.tile([P, 2 * H], U8, name="w4_raw")
        w4_raw_scales = keep.tile([P, H], U8, name="w4_raw_scales")
        w4_codes = keep.tile([P, 2 * H], U8, name="w4_codes", align_bytes=64)
        w4_plane = keep.tile([P, H], U8, name="w4_plane", align_bytes=64)
        pick_words = [[keep.tile([P, COLS], U32, name="pick%d_%d" % (a, c), align_bytes=64) for c in range(2)] for a in range(2)]
        pick2_words = keep.tile([P, S], U32, name="pick2_words", align_bytes=64)
        pick_scales = keep.tile([P, S], U8, name="pick_scales", align_bytes=64)
        pick2_scales = keep.tile([P, S], U8, name="pick2_scales", align_bytes=64)
        phi_sb = keep.tile([P, 2, PACK], F32, name="phi_sb")
        neg_phi = keep.tile([P, 2, PACK], F32, name="neg_phi")
        b_sb = keep.tile([P, 2, PACK], F32, name="b_sb")
        p0_sb = keep.tile([P, 2, PACK], F32, name="p0_sb")
        y_plane = keep.tile([P, 2, S], U8, name="y_plane", align_bytes=64)

        def weight_tiles(label):
            raw, codes, plane = {}, {}, {}
            for g in range(2):
                for a in range(2):
                    raw[g, a] = keep.tile([P, PACK, GROUP], F32, name="%s_raw%d%d" % (label, g, a))
                    codes[g, a] = keep.tile([P, GROUP], U32, name="%s_codes%d%d" % (label, g, a), align_bytes=64)
                    plane[g, a] = keep.tile([P, GROUP], U8, name="%s_plane%d%d" % (label, g, a), align_bytes=64)
            return raw, codes, plane

        w1_raw, w1_codes, w1_plane = weight_tiles("w1")
        wi_raw, wi_codes, wi_plane = weight_tiles("wi")
        h_codes = {}
        h_plane = {}
        for g in range(2):
            for c in range(2):
                h_codes[g, c] = keep.tile([P, COLS], U32, name="h_codes%d%d" % (g, c), align_bytes=64)
                h_plane[g, c] = keep.tile([P, COLS], U8, name="h_plane%d%d" % (g, c), align_bytes=64)

        def load_words(dst, src):
            nc.sync.dma_start(out=dst[:].bitcast(I32), in_=src.rearrange("p t i -> p (t i)").bitcast(I32))

        def load_weight(raw, w, g, a):
            rows = w[a * GROUP : (a + 1) * GROUP, g * GROUP : (g + 1) * GROUP]
            nc.sync.dma_start(out=raw[g, a][:], in_=rows.rearrange("(p j) c -> p j c", j=PACK))

        def load_dealt(dst, vec):
            nc.sync.dma_start(out=dst[:], in_=vec.rearrange("(g p t) -> p g t", g=2, t=PACK))

        def load_scale_rows(queue, dst, src):
            passes = src.shape[0]
            for q in range(QUADS):
                queue.dma_start(
                    out=dst[32 * q : 32 * q + 4 * passes, :].bitcast(I32),
                    in_=src[:, 4 * q : 4 * q + 4, :].bitcast(I32),
                )

        def gather(dst, window, offsets):
            nc.vector.tensor_copy(out=dst, in_=window[:].indirect(offsets))

        def half(lst, c):
            return lst[:, c * (COLS // LIST_ROWS) : (c + 1) * (COLS // LIST_ROWS)]

        def quantise(codes, plane, grouped):
            nc.vector.quantize_mx(out=codes.bitcast(FP8X4), scales=plane, in_=grouped[:])

        def round_weight(raw, on_scalar, negate):
            grouped = ring.tile([P, PACK * GROUP], BF16, name="w_grouped", align_bytes=64, bufs=3)
            dst = grouped[:].rearrange("p (t m j) -> p m j t", t=PACK, j=PACK)
            src = raw[:].rearrange("p j (m t) -> p m j t", t=PACK)
            if on_scalar and negate:
                nc.scalar.activation(out=dst, in_=src, func=ACT.Copy, scale=-1.0)
            elif on_scalar:
                nc.scalar.copy(out=dst, in_=src)
            elif negate:
                nc.vector.tensor_scalar(out=dst, in0=src, scalar1=-1.0, scalar2=None, op0=ALU.mult)
            else:
                nc.vector.tensor_copy(out=dst, in_=src)
            return grouped

        def prepare_w1(g, a, on_scalar):
            quantise(w1_codes[g, a][:], w1_plane[g, a][:], round_weight(w1_raw[g, a], on_scalar, True))

        def prepare_wi(g, a, on_scalar):
            quantise(wi_codes[g, a][:], wi_plane[g, a][:], round_weight(wi_raw[g, a], on_scalar, False))

        def woven(ap):
            return ap.rearrange("p (c i t) -> p c t i", i=PACK, t=PACK)

        def by_lines(ap):
            return ap.rearrange("p t (c i) -> p c t i", i=PACK)

        def angles(g, c):
            cols = slice(c * COLS, (c + 1) * COLS)
            banks = [psum.tile([P, COLS], F32, name="acc") for t in range(PACK)]
            for t in range(PACK):
                e = (PACK * g + t) * P
                nc.tensor.matmul_mx(
                    out=banks[t][:],
                    lhsT=w4_codes[:, 2 * e : 2 * (e + P)].bitcast(FP4X4),
                    lhsT_scale=w4_plane[:, e : e + P],
                    rhs=pick2_words[:, cols].bitcast(FP8X4),
                    rhs_scale=pick2_scales[:, cols],
                    start=True,
                    stop=False,
                )
            for a in range(2):
                for t in range(PACK):
                    nc.tensor.matmul_mx(
                        out=banks[t][:],
                        lhsT=w1_codes[g, a][:, t * P : (t + 1) * P].bitcast(FP8X4),
                        lhsT_scale=w1_plane[g, a][:, t * P : (t + 1) * P],
                        rhs=pick_words[a][c][:].bitcast(FP8X4),
                        rhs_scale=pick_scales[4 * a : P, cols],
                        start=False,
                        stop=(a == 1),
                    )
            sines = ring.tile([P, PACK, COLS], F32, name="sines", bufs=3)
            for t in range(PACK):
                nc.scalar.activation(
                    out=sines[:, t, :], in_=banks[t][:], func=ACT.Sin, scale=-1.0, bias=neg_phi[:, g, t : t + 1]
                )
            return sines

        def powers(g, c, sines):
            grouped = ring.tile([P, PACK * COLS], BF16, name="h_grouped", align_bytes=64)
            strength = b_sb[:, g, :].unsqueeze(1).unsqueeze(3).to_broadcast([P, COLS // PACK, PACK, PACK])
            nc.vector.tensor_tensor(out=woven(grouped[:]), in0=by_lines(sines[:]), in1=strength, op=ALU.mult)
            quantise(h_codes[g, c][:], h_plane[g, c][:], grouped)

        def injections(g, c):
            cols = slice(c * COLS, (c + 1) * COLS)
            y = ring.tile([P, PACK, COLS], F32, name="y", bufs=3)
            rows = out_0[g * GROUP : (g + 1) * GROUP, cols].rearrange("(p t) j -> p t j", t=PACK)
            for t in range(PACK):
                bank = psum.tile([P, COLS], F32, name="acc")
                for a in range(2):
                    nc.tensor.matmul_mx(
                        out=bank[:],
                        lhsT=wi_codes[g, a][:, t * P : (t + 1) * P].bitcast(FP8X4),
                        lhsT_scale=wi_plane[g, a][:, t * P : (t + 1) * P],
                        rhs=h_codes[a, c][:].bitcast(FP8X4),
                        rhs_scale=h_plane[a, c][:],
                        start=(a == 0),
                        stop=(a == 1),
                    )
                nc.scalar.activation(out=y[:, t, :], in_=bank[:], func=ACT.Identity, bias=p0_sb[:, g, t : t + 1])
                nc.sync.dma_start(out=rows[:, t, :], in_=y[:, t, :])
            return y

        def planes(g, c, y):
            cols = slice(c * COLS, (c + 1) * COLS)
            grouped = ring.tile([P, PACK * COLS], BF16, name="y_grouped", align_bytes=64)
            nc.vector.tensor_copy(out=woven(grouped[:]), in_=by_lines(y[:]))
            codes = ring.tile([P, COLS], U32, name="y_codes", align_bytes=64)
            quantise(codes[:], y_plane[:, g, cols], grouped)
            dst = out_1[g, :, cols, :].rearrange("p m t -> p (m t)").bitcast(I32)
            nc.sync.dma_start(out=dst, in_=codes[:].bitcast(I32))

        nc.gpsimd.memset(v_scales[:].bitcast(I32), 0)
        for plane in (v2_scales, w4_raw_scales):
            nc.vector.memset(plane[:].bitcast(I32), 0)
        load_scale_rows(nc.scalar, v2_scales, tab2_scales)
        load_scale_rows(nc.scalar, v_scales, tab_scales)

        nc.sync.dma_start(list2[:], offs2)
        nc.sync.dma_start(list1[:], offs)
        load_dealt(phi_sb, phi)
        load_dealt(b_sb, b)
        load_dealt(p0_sb, p0)
        nc.sync.dma_start(out=w4_raw[:].bitcast(I32), in_=w4_words[0].bitcast(I32))
        load_weight(w1_raw, w1, 0, 0)
        load_weight(w1_raw, w1, 0, 1)
        load_words(v2_words, tab2_words[0])
        load_scale_rows(nc.sync, w4_raw_scales, w4_scales)
        load_words(v_words[0], tab_words[0])
        load_words(v_words[1], tab_words[1])
        load_weight(w1_raw, w1, 1, 0)
        load_weight(w1_raw, w1, 1, 1)
        load_weight(wi_raw, wi, 0, 0)
        load_weight(wi_raw, wi, 0, 1)
        load_weight(wi_raw, wi, 1, 0)
        load_weight(wi_raw, wi, 1, 1)

        gather(pick2_scales[:], v2_scales, list2[:])
        nc.vector.tensor_copy(
            out=w4_codes[:].bitcast(U16).rearrange("p (g t m) -> p g t m", g=2, t=PACK),
            in_=w4_raw[:].bitcast(U16).rearrange("p (g m t) -> p g t m", g=2, t=PACK),
        )
        nc.vector.tensor_scalar(out=neg_phi[:], in0=phi_sb[:], scalar1=-1.0, scalar2=None, op0=ALU.mult)
        prepare_w1(0, 0, True)
        gather(pick_scales[:], v_scales, list1[:])
        prepare_w1(0, 1, True)
        gather(pick2_words[:], v2_words, list2[:])
        nc.vector.tensor_copy(
            out=w4_plane[:].rearrange("p (g t m) -> p g t m", g=2, t=PACK),
            in_=w4_raw_scales[:].rearrange("p (g m t) -> p g t m", g=2, t=PACK),
        )
        for a in range(2):
            for c in range(2):
                gather(pick_words[a][c][:], v_words[a], half(list1, c))

        s00 = angles(0, 0)
        s01 = angles(0, 1)
        prepare_w1(1, 0, False)
        prepare_w1(1, 1, False)
        s10 = angles(1, 0)
        powers(0, 0, s00)
        powers(0, 1, s01)
        prepare_wi(0, 0, True)
        s11 = angles(1, 1)
        powers(1, 0, s10)
        prepare_wi(0, 1, True)
        powers(1, 1, s11)
        prepare_wi(1, 0, True)
        y00 = injections(0, 0)
        prepare_wi(1, 1, False)
        y01 = injections(0, 1)
        planes(0, 0, y00)
        y10 = injections(1, 0)
        planes(0, 1, y01)
        y11 = injections(1, 1)
        planes(1, 0, y10)
        planes(1, 1, y11)
        for q in range(QUADS):
            nc.sync.dma_start(
                out=out_2[:, 4 * q : 4 * q + 4, :].rearrange("g r m -> r g m").bitcast(I32),
                in_=y_plane[32 * q : 32 * q + 4, :, :].bitcast(I32),
            )
